import numpy as np
import ml_dtypes


def mxq(x, axis, fmt="e4m3"):
    dtype, down = {"e4m3": (ml_dtypes.float8_e4m3fn, 7), "e5m2": (ml_dtypes.float8_e5m2, 14)}[fmt]
    v = np.moveaxis(np.asarray(x, np.float32).astype(ml_dtypes.bfloat16).astype(np.float64), axis, -1)
    blocks = v.reshape(v.shape[:-1] + (-1, 32))
    amax = np.abs(blocks).max(-1, keepdims=True)
    byte = np.maximum(np.where(amax > 0, np.frexp(amax)[1] - 1 + 127, 0) - down, 1)
    scale = np.exp2(byte - 127.0)
    codes = (blocks / scale).astype(np.float32).astype(dtype).astype(np.float64)
    return np.moveaxis((codes * scale).reshape(v.shape), -1, axis)


WIDE = False


def mx_kscale(k):
    if not WIDE:
        return np.ones(k)
    levels = np.array([10, -10, 5, -5, 0])
    if k % 512:
        return np.exp2(np.random.permutation(np.resize(levels, k // 32))).repeat(32)
    a = np.empty((k // 512, 16))
    for p in range(k // 512):
        a[p, :8] = np.random.permutation(np.resize(levels, 8))
        for g in range(8):
            far = levels[np.abs(levels - a[p, g]) >= 10]
            a[p, g + 8] = far[np.random.randint(len(far))]
    return np.exp2(a.ravel()).repeat(32)


BF16 = ml_dtypes.bfloat16


def bf(x):
    return np.asarray(x, np.float32).astype(BF16)


def f64(x):
    return np.asarray(x).astype(np.float64)


E2M1 = np.array([0.0, 0.5, 1.0, 1.5, 2.0, 3.0, 4.0, 6.0, -0.0, -0.5, -1.0, -1.5, -2.0, -3.0, -4.0, -6.0])


def pack_weight(w, fmt):
    k, n = w.shape
    w = f64(bf(w)).reshape(k // 32, 32, n)
    amax = np.abs(w).max(1)
    if fmt == "e4m3":
        byte = np.frexp(amax)[1] - 1 + 127 - 7
    else:
        mant, ex = np.frexp(amax / 6.0)
        byte = np.where(mant > 0.5, ex, ex - 1) + 127
    byte = np.clip(np.where(amax > 0, byte, 1), 1, 254)
    scaled = (w * np.exp2(127.0 - byte)[:, None, :]).reshape(k, n).astype(np.float32)
    by_word = np.ascontiguousarray(scaled.reshape(k // 512, 128, 4, n).transpose(0, 1, 3, 2))
    if fmt == "e4m3":
        words = by_word.astype(ml_dtypes.float8_e4m3fn).view(np.uint8)
    else:
        c = by_word.astype(ml_dtypes.float4_e2m1fn).view(np.uint8) & 0xF
        words = c[..., 0::2] | (c[..., 1::2] << 4)
    return np.ascontiguousarray(words), np.ascontiguousarray(byte.astype(np.uint8).reshape(k // 512, 16, n))


def unpack_weight(words, scales, fmt):
    g, p, n, _ = words.shape
    if fmt == "e4m3":
        vals = np.ascontiguousarray(words).view(ml_dtypes.float8_e4m3fn).astype(np.float64)
    else:
        nib = np.empty((g, p, n, 4), np.uint8)
        nib[..., 0::2] = words & 0xF
        nib[..., 1::2] = words >> 4
        vals = E2M1[nib]
    vals = vals * np.repeat(np.exp2(scales.astype(np.float64) - 127.0), 8, axis=1)[..., None]
    return vals.transpose(0, 1, 3, 2).reshape(g * 512, n)

E4M3FN = np.array([(-1.0 if i & 128 else 1.0) * ((1.0 + (i & 7) / 8.0) * 2.0 ** (((i >> 3) & 15) - 7) if i & 120 else (i & 7) * 2.0 ** -9) for i in range(256)])


def e4m3fn_bytes(y):
    return np.clip(np.asarray(y, np.float64), -448.0, 448.0).astype(np.float32).astype(ml_dtypes.float8_e4m3fn).view(np.uint8)


def e4m3fn_values(b):
    return E4M3FN[b]


B, D, F, O, A = 1024, 1024, 1024, 128, 8
P = O * A


def option_action_view(flat, n_options):
    n_rows, n_cols = flat.shape
    return flat.reshape(n_rows, n_options, n_cols // n_options)


def softmax_last(v):
    e = np.exp(v - v.max(axis=-1, keepdims=True))
    return e / e.sum(axis=-1, keepdims=True)


def sigmoid(v):
    return 1.0 / (1.0 + np.exp(-v))


def draw0():
    s, t = mx_kscale(D), mx_kscale(F)
    x = bf(np.random.standard_normal((B, D)) * s)
    w0_words, w0_scales = pack_weight(np.random.standard_normal((D, F)) / np.sqrt(D) / s[:, None], "e4m3")
    gf = bf((1.0 + 0.1 * np.random.standard_normal(F)) * t)
    wq_words, wq_scales = pack_weight(np.random.standard_normal((F, P)) * 1.5 / np.sqrt(F) / t[:, None], "e4m3")
    wp_words, wp_scales = pack_weight(np.random.standard_normal((F, P)) * 2.0 / np.sqrt(F) / t[:, None], "e4m3")
    wb_words, wb_scales = pack_weight(np.random.standard_normal((F, O)) * 1.5 / np.sqrt(F) / t[:, None], "e4m3")
    bb = bf(np.random.standard_normal(O) * 0.5)
    return {
        "x": x,
        "w0_words": w0_words,
        "w0_scales": w0_scales,
        "gf": gf,
        "wq_words": wq_words,
        "wq_scales": wq_scales,
        "wp_words": wp_words,
        "wp_scales": wp_scales,
        "wb_words": wb_words,
        "wb_scales": wb_scales,
        "bb": bb,
    }


def core(x, w0_words, w0_scales, gf, wq_words, wq_scales, wp_words, wp_scales, wb_words, wb_scales, bb):
    n_options = bb.shape[0]

    f = np.tanh(mxq(f64(x), 1, "e4m3") @ unpack_weight(w0_words, w0_scales, "e4m3")) * f64(gf)[None, :]
    fq = mxq(f, 1, "e4m3")

    qu = option_action_view(fq @ unpack_weight(wq_words, wq_scales, "e4m3"), n_options)

    pi = softmax_last(option_action_view(fq @ unpack_weight(wp_words, wp_scales, "e4m3"), n_options))

    qo = np.sum(pi * qu, axis=-1)

    beta = sigmoid((fq @ unpack_weight(wb_words, wb_scales, "e4m3")) + f64(bb)[None, :])

    vmax = np.max(qo, axis=-1, keepdims=True)

    return (1.0 - beta) * qo + beta * vmax


def setup_inputs():
    drawn = draw0()
    full = np.asarray(drawn['x']).astype(np.float64)
    scale = (np.abs(full).reshape(8, 128, 8, 128).max(axis=(1, 3)) / 448.0).astype(np.float32)
    given = {}
    for key, value in drawn.items():
        if key == 'x':
            given['x_bytes'] = e4m3fn_bytes(full / np.repeat(np.repeat(scale.astype(np.float64), 128, axis=0), 128, axis=1))
            given['x_scale'] = scale
        else:
            given[key] = value
    return given


def reference(x_bytes, x_scale, w0_words, w0_scales, gf, wq_words, wq_scales, wp_words, wp_scales, wb_words, wb_scales, bb):
    return core(e4m3fn_values(x_bytes) * np.repeat(np.repeat(x_scale.astype(np.float64), 128, axis=0), 128, axis=1), w0_words, w0_scales, gf, wq_words, wq_scales, wp_words, wp_scales, wb_words, wb_scales, bb)

@@ -1,0 +1,670 @@
+from contextlib import ExitStack
+
+import concourse.mybir as mybir
+from concourse.masks import make_identity
+
+F32 = mybir.dt.float32
+BF16 = mybir.dt.bfloat16
+I32 = mybir.dt.int32
+U32 = mybir.dt.uint32
+U8 = mybir.dt.uint8
+FP8 = mybir.dt.float8_e4m3fn
+FP8X4 = mybir.dt.float8_e4m3fn_x4
+ALU = mybir.AluOpType
+ACT = mybir.ActivationFunctionType
+AX = mybir.AxisListType
+
+P = 128
+B = 1024
+D = 1024
+F = 1024
+O = 128
+A = 8
+HALF = 512
+NT = B // P
+FLOPS = 2 * B * D * F + 2 * B * F * (2 * O * A + O)
+
+WIDEN = 'VVVVVVVV'
+EVAC = 'VSVSSSSS'
+XTAG = 'qqsoqqso'
+BUFS = {'z': 3, 'q': 2, 's': 2, 'o': 1}
+FTAG = ('z', 's')
+BTAG = 'o'
+EQG = (4, 5, 6, 7, 8, 9, 10, 11, 12, 13)
+GROUPS = {0: (0, 4, 'ln'), 4: (4, 2, 'v'), 6: (6, 1, 'v'), 7: (7, 1, 'v')}
+BANK_OF = {0: (0, 0), 1: (0, 1), 2: (2, 0), 3: (2, 1), 4: (4, 0), 5: (4, 1), 6: (6, 0), 7: (7, 0)}
+GAIN = {(0, 0, 0): 'V', (0, 0, 1): 'G', (0, 1, 0): 'V', (0, 1, 1): 'G', (1, 0, 0): 'G', (1, 0, 1): 'G', (1, 1, 0): 'V', (1, 1, 1): 'G'}
+PLAN = [
+    ('widen', (0,)),
+    ('widen', (1,)),
+    ('turn', (0,)),
+    ('pick', ()),
+    ('widen', (2,)),
+    ('turn', (1,)),
+    ('evac', (0, 0)),
+    ('evac', (1, 0)),
+    ('widen', (3,)),
+    ('evac', (0, 1)),
+    ('turn', (3,)),
+    ('permW', (0,)),
+    ('evac', (3, 0)),
+    ('widen', (5,)),
+    ('evac', (3, 1)),
+    ('widen', (6,)),
+    ('turn', (5,)),
+    ('evac', (1, 1)),
+    ('widen', (7,)),
+    ('turn', (2,)),
+    ('evac', (5, 0)),
+    ('widen', (4,)),
+    ('turn', (6,)),
+    ('evac', (5, 1)),
+    ('evac', (2, 0)),
+    ('turn', (7,)),
+    ('evac', (6, 0)),
+    ('permS', (0,)),
+    ('turn', (4,)),
+    ('evac', (7, 0)),
+    ('evac', (2, 1)),
+    ('evac', (4, 0)),
+    ('quantx', (0, 0)),
+    ('evac', (7, 1)),
+    ('quantx', (0, 1)),
+    ('evac', (6, 1)),
+    ('permS', (1,)),
+    ('mmf', (0, 0, 1)),
+    ('evac', (4, 1)),
+    ('permW', (1,)),
+    ('mmf', (0, 0, 0)),
+    ('tanh', (0, 0, 1)),
+    ('quantx', (1, 0)),
+    ('mmf', (0, 1, 0)),
+    ('tanh', (0, 0, 0)),
+    ('quantx', (1, 1)),
+    ('mmf', (0, 0, 2)),
+    ('tanh', (0, 1, 0)),
+    ('mmf', (0, 0, 3)),
+    ('tanh', (0, 0, 2)),
+    ('mmf', (0, 1, 3)),
+    ('tanh', (0, 0, 3)),
+    ('mmf', (0, 1, 1)),
+    ('tanh', (0, 1, 3)),
+    ('gain', (0, 0, 0)),
+    ('gain', (0, 0, 1)),
+    ('mmf', (0, 1, 2)),
+    ('tanh', (0, 1, 1)),
+    ('mmf', (1, 0, 0)),
+    ('tanh', (0, 1, 2)),
+    ('quantf', (0, 0, 0)),
+    ('mmf', (1, 0, 2)),
+    ('tanh', (1, 0, 0)),
+    ('gain', (0, 1, 0)),
+    ('tanh', (1, 0, 2)),
+    ('mmf', (1, 0, 3)),
+    ('gain', (0, 1, 1)),
+    ('mmf', (1, 0, 1)),
+    ('quantf', (0, 1, 0)),
+    ('tanh', (1, 0, 3)),
+    ('mmz', (0,)),
+    ('tanh', (1, 0, 1)),
+    ('mmf', (1, 1, 2)),
+    ('max', (0,)),
+    ('mmz', (3,)),
+    ('gain', (1, 0, 0)),
+    ('tanh', (1, 1, 2)),
+    ('quantf', (0, 0, 1)),
+    ('quantf', (0, 1, 1)),
+    ('mmf', (1, 1, 1)),
+    ('max', (3,)),
+    ('mmz', (5,)),
+    ('tanh', (1, 1, 1)),
+    ('sub', (0,)),
+    ('mmf', (1, 1, 0)),
+    ('sub', (3,)),
+    ('mmz', (4,)),
+    ('gain', (1, 0, 1)),
+    ('tanh', (1, 1, 0)),
+    ('max', (5,)),
+    ('mmf', (1, 1, 3)),
+    ('exp', (0,)),
+    ('max', (4,)),
+    ('mmq', (5,)),
+    ('tanh', (1, 1, 3)),
+    ('sub', (4,)),
+    ('mmq', (7,)),
+    ('qcp', (5,)),
+    ('quantf', (1, 0, 0)),
+    ('mmz', (1,)),
+    ('gain', (1, 1, 0)),
+    ('qcp', (7,)),
+    ('gain', (1, 1, 1)),
+    ('mmq', (4,)),
+    ('exp', (3,)),
+    ('mmb', (0,)),
+    ('max', (1,)),
+    ('qcp', (4,)),
+    ('mmq', (6,)),
+    ('sub', (5,)),
+    ('mmq', (0,)),
+    ('quantf', (1, 1, 0)),
+    ('qcp', (6,)),
+    ('quantf', (1, 1, 1)),
+    ('mmz', (2,)),
+    ('sub', (1,)),
+    ('exp', (5,)),
+    ('mmz', (6,)),
+    ('max', (2,)),
+    ('exp', (4,)),
+    ('mmz', (9,)),
+    ('mul', (0,)),
+    ('bcp', (0,)),
+    ('mul', (4,)),
+    ('mmq', (8,)),
+    ('sub', (2,)),
+    ('mmq', (3,)),
+    ('qcp', (8,)),
+    ('max', (6,)),
+    ('mmz', (8,)),
+    ('exp', (1,)),
+    ('sub', (6,)),
+    ('mmq', (1,)),
+    ('mul', (3,)),
+    ('exp', (6,)),
+    ('mmz', (7,)),
+    ('max', (9,)),
+    ('sume', (2,)),
+    ('mul', (6,)),
+    ('max', (8,)),
+    ('sume', (0,)),
+    ('sub', (9,)),
+    ('mul', (5,)),
+    ('mmq', (11,)),
+    ('sub', (8,)),
+    ('quantf', (1, 0, 1)),
+    ('mmz', (10,)),
+    ('exp', (8,)),
+    ('max', (7,)),
+    ('mmb', (1,)),
+    ('qcp', (11,)),
+    ('mul', (8,)),
+    ('sub', (7,)),
+    ('mmz', (12,)),
+    ('exp', (9,)),
+    ('mul', (1,)),
+    ('mmz', (11,)),
+    ('exp', (7,)),
+    ('max', (10,)),
+    ('mmq', (9,)),
+    ('exp', (2,)),
+    ('sub', (10,)),
+    ('sume', (3,)),
+    ('bcp', (1,)),
+    ('max', (12,)),
+    ('exp', (10,)),
+    ('sume', (1,)),
+    ('bbias', (1,)),
+    ('max', (11,)),
+    ('qcp', (9,)),
+    ('mmz', (15,)),
+    ('sub', (12,)),
+    ('ln', (0,)),
+    ('bbias', (0,)),
+    ('sub', (11,)),
+    ('mmq', (2,)),
+    ('mmz', (14,)),
+    ('mul', (2,)),
+    ('mmz', (13,)),
+    ('mul', (7,)),
+    ('max', (15,)),
+    ('sumq', (1,)),
+    ('btanh', (0,)),
+    ('max', (13,)),
+    ('sumq', (0,)),
+    ('sub', (13,)),
+    ('max', (14,)),
+    ('sumq', (3,)),
+    ('sub', (15,)),
+    ('sumq', (2,)),
+    ('rexp', (0,)),
+    ('baff', (0,)),
+    ('mmq', (10,)),
+    ('exp', (11,)),
+    ('qmul', (0,)),
+    ('mul', (9,)),
+    ('mmq', (12,)),
+    ('exp', (12,)),
+    ('sub', (14,)),
+    ('fturn', (0,)),
+    ('qcp', (10,)),
+    ('sume', (4,)),
+    ('mul', (11,)),
+    ('fmax', (0,)),
+    ('exp', (13,)),
+    ('sume', (5,)),
+    ('qcp', (12,)),
+    ('mix', (0,)),
+    ('mul', (10,)),
+    ('sume', (6,)),
+    ('exp', (15,)),
+    ('recip', (4,)),
+    ('mmq', (13,)),
+    ('mul', (12,)),
+    ('sumq', (5,)),
+    ('qcp', (13,)),
+    ('btanh', (1,)),
+    ('sumq', (4,)),
+    ('mul', (13,)),
+    ('recip', (6,)),
+    ('exp', (14,)),
+    ('mmq', (14,)),
+    ('fout', (0,)),
+    ('mmq', (15,)),
+    ('qmul', (4,)),
+    ('baff', (1,)),
+    ('mul', (14,)),
+    ('fturn', (4,)),
+    ('sumq', (6,)),
+    ('mul', (15,)),
+    ('fmax', (4,)),
+    ('sume', (7,)),
+    ('mix', (4,)),
+    ('sumq', (7,)),
+    ('qmul', (6,)),
+    ('recip', (7,)),
+    ('fturn', (6,)),
+    ('fmax', (6,)),
+    ('qmul', (7,)),
+    ('mix', (6,)),
+    ('fturn', (7,)),
+    ('fout', (6,)),
+    ('fout', (4,)),
+    ('fmax', (7,)),
+    ('mix', (7,)),
+    ('fout', (7,)),
+]
+
+
+def tile_optioncriticuponarrivalvalue_d2p_kernel(
+    tc, x_bytes, x_scale, w0_words, w0_scales, gf, wq_words, wq_scales, wp_words, wp_scales, wb_words, wb_scales, bb, out
+):
+    nc = tc.nc
+    with ExitStack() as ctx:
+        keep = ctx.enter_context(tc.tile_pool(name="keep", bufs=1))
+        work = ctx.enter_context(tc.tile_pool(name="work", bufs=2))
+        psum = ctx.enter_context(tc.psum_pool(name="psum", bufs=1))
+
+        xsc = keep.tile([P, 64], F32, name="xsc")
+        xsp = keep.tile([P, 2, NT], F32, name="xsp")
+        w0w = keep.tile([P, 2, F], I32, name="w0w", align_bytes=64)
+        w0p = keep.tile([P, 2, F], I32, name="w0p", align_bytes=64)
+        w0s = keep.tile([P, F], U8, name="w0s", align_bytes=64)
+        w0sp = keep.tile([P, F], U8, name="w0sp", align_bytes=64)
+        gft = keep.tile([P, 2, 4], BF16, name="gft")
+        bbt = keep.tile([P, O], BF16, name="bbt")
+        wpw = keep.tile([P, 2, O * A], I32, name="wpw", align_bytes=64)
+        wqw = keep.tile([P, 2, O * A], I32, name="wqw", align_bytes=64)
+        wps = keep.tile([P, O * A], U8, name="wps", align_bytes=64)
+        wqs = keep.tile([P, O * A], U8, name="wqs", align_bytes=64)
+        wbw = keep.tile([P, 2, O], I32, name="wbw", align_bytes=64)
+        wbs = keep.tile([P, O], U8, name="wbs", align_bytes=64)
+        ident = keep.tile([P, P], F32, name="ident")
+        xqw = keep.tile([P, 2, B], U32, name="xqw", align_bytes=64)
+        xqs = keep.tile([P, 2, B], U8, name="xqs", align_bytes=64)
+        fqw = keep.tile([P, 2, B], U32, name="fqw", align_bytes=64)
+        fqs = keep.tile([P, 2, B], U8, name="fqs", align_bytes=64)
+        beta = keep.tile([P, NT, O], F32, name="beta")
+        dummy = keep.tile([P, 1], F32, name="dummy")
+        xb = [keep.tile([P, D], U8, name="xb%d" % i) for i in range(NT)]
+
+        ctx.enter_context(tc.manual_schedule())
+
+        nc.vector.memset(dummy[:], 0.0)
+        nc.scalar.activation(out=dummy[:], in_=dummy[:], func=ACT.Exp)
+        nc.vector.memset(w0s[:].bitcast(I32), 0)
+        make_identity(nc, ident[:])
+        nc.gpsimd.memset(wps[:].bitcast(I32), 0)
+        nc.gpsimd.memset(wqs[:].bitcast(I32), 0)
+        nc.gpsimd.memset(wbs[:].bitcast(I32), 0)
+
+        def load_x(i):
+            nc.sync.dma_start(out=xb[i][:], in_=x_bytes[i * P : (i + 1) * P, :])
+
+        def load_scales(dst, src):
+            for q in range(4):
+                nc.sync.dma_start(
+                    out=dst[32 * q : 32 * q + 8, :].bitcast(I32),
+                    in_=src[:, 4 * q : 4 * q + 4, :].bitcast(I32),
+                )
+
+        def load_words(dst, src, g, c0, c1):
+            nc.sync.dma_start(
+                out=dst[:, g, c0:c1],
+                in_=src[g].rearrange("p n t -> p (n t)")[:, 4 * c0 : 4 * c1].bitcast(I32),
+            )
+
+        load_x(0)
+        nc.sync.dma_start(out=xsc[:], in_=x_scale.rearrange("i j -> (i j)").partition_broadcast(P))
+        for i in range(1, 4):
+            load_x(i)
+        load_scales(w0s, w0_scales)
+        for g in range(2):
+            load_words(w0w, w0_words, g, 0, HALF)
+        nc.sync.dma_start(out=gft[:], in_=gf.rearrange("(g p t) -> p g t", p=P, t=4))
+        load_scales(wps, wp_scales)
+        load_scales(wqs, wq_scales)
+        load_scales(wbs, wb_scales)
+        for i in range(4, NT):
+            load_x(i)
+        for g in range(2):
+            load_words(w0w, w0_words, g, HALF, F)
+        for c in range(2):
+            for g in range(2):
+                load_words(wpw, wp_words, g, c * HALF, (c + 1) * HALF)
+            for g in range(2):
+                load_words(wqw, wq_words, g, c * HALF, (c + 1) * HALF)
+        for g in range(2):
+            load_words(wbw, wb_words, g, 0, O)
+        nc.sync.dma_start(out=bbt[:], in_=bb.partition_broadcast(P))
+
+        def bank(tag):
+            return psum.tile([P, HALF], F32, name="ps_" + tag, tag=tag, bufs=BUFS[tag])
+
+        xwide, xbank, xt = {}, {}, {}
+        for h in range(2):
+            for g in range(2):
+                xt[h, g] = keep.tile([P, HALF, 4], BF16, name="xt%d%d" % (h, g), align_bytes=64)
+
+        def pick():
+            for q in range(4):
+                nc.vector.tensor_copy(
+                    out=xsp[32 * q : 32 * q + 32, :, :],
+                    in_=xsc[32 * q : 32 * q + 32, :].rearrange("p (i g q) -> p q g i", g=2, q=4)[:, q],
+                )
+
+        def widen(i):
+            t = work.tile([P, D], BF16, name="xw", tag="xw", bufs=8, align_bytes=64)
+            src = xb[i][:].bitcast(FP8)
+            if WIDEN[i] == "V":
+                nc.vector.tensor_copy(out=t[:], in_=src)
+            else:
+                nc.scalar.copy(out=t[:], in_=src)
+            xwide[i] = t
+
+        def turn(i):
+            bk = bank(XTAG[i])
+            words = xwide[i][:].bitcast(F32)
+            for g in range(2):
+                for u in range(2):
+                    j = 2 * g + u
+                    nc.tensor.transpose(
+                        bk[:, j * P : (j + 1) * P], words[:, 256 * g + u : 256 * (g + 1) : 2], ident[:]
+                    )
+            xbank[i] = bk
+
+        def evac(i, g):
+            r0 = (i % 4) * P
+            src = xbank[i][:, g * 256 : (g + 1) * 256].bitcast(BF16).rearrange("p (u r e) -> p r u e", u=2, e=2)
+            dst = xt[i // 4, g][:, r0 : r0 + P, :].rearrange("p r (u e) -> p r u e", e=2)
+            if EVAC[i] == "V":
+                nc.vector.tensor_scalar(
+                    out=dst, in0=src, scalar1=xsp[:, g, i : i + 1], scalar2=None, op0=ALU.mult
+                )
+            else:
+                nc.scalar.activation(out=dst, in_=src, func=ACT.Copy, scale=xsp[:, g, i : i + 1])
+
+        def quantx(h, g):
+            nc.vector.quantize_mx(
+                out=xqw[:, g, h * HALF : (h + 1) * HALF].bitcast(FP8X4),
+                scales=xqs[:, g, h * HALF : (h + 1) * HALF],
+                in_=xt[h, g][:].rearrange("p r t -> p (r t)"),
+            )
+
+        def permW(G):
+            nc.vector.tensor_copy(
+                out=w0p[:, :, G * HALF : (G + 1) * HALF].rearrange("p g (t m) -> p g t m", t=4),
+                in_=w0w[:, :, G * HALF : (G + 1) * HALF].rearrange("p g (m t) -> p g t m", t=4),
+            )
+
+        def permS(G):
+            nc.vector.tensor_copy(
+                out=w0sp[:, G * HALF : (G + 1) * HALF].rearrange("p (t m) -> p t m", t=4),
+                in_=w0s[:, G * HALF : (G + 1) * HALF].rearrange("p (m t) -> p t m", t=4),
+            )
+
+        fbank, th, fb = {}, {}, {}
+
+        def mmf(h, G, t):
+            bk = bank(FTAG[h])
+            c0 = G * HALF + t * P
+            for g in range(2):
+                nc.tensor.matmul_mx(
+                    out=bk[:],
+                    lhsT=w0p[:, g, c0 : c0 + P].bitcast(FP8X4),
+                    lhsT_scale=w0sp[4 * g : P, c0 : c0 + P],
+                    rhs=xqw[:, g, h * HALF : (h + 1) * HALF].bitcast(FP8X4),
+                    rhs_scale=xqs[:, g, h * HALF : (h + 1) * HALF],
+                    start=(g == 0),
+                    stop=(g == 1),
+                )
+            fbank[h, G, t] = bk
+
+        def tanh(h, G, t):
+            if (h, G) not in th:
+                th[h, G] = work.tile([P, 4, HALF], F32, name="th", tag="th", bufs=4)
+            nc.scalar.activation(out=th[h, G][:, t, :], in_=fbank[h, G, t][:], func=ACT.Tanh)
+
+        def gain(h, G, c):
+            c0, c1 = 256 * c, 256 * (c + 1)
+            if (h, G) not in fb:
+                fb[h, G] = work.tile([P, HALF, 4], BF16, name="fb", tag="fb", bufs=4, align_bytes=64)
+            eng = nc.vector if GAIN[h, G, c] == "V" else nc.gpsimd
+            eng.tensor_tensor(
+                out=fb[h, G][:, c0:c1, :],
+                in0=th[h, G][:, :, c0:c1].rearrange("p t c -> p c t"),
+                in1=gft[:, G : G + 1, :].to_broadcast([P, c1 - c0, 4]),
+                op=ALU.mult,
+            )
+
+        def quantf(h, G, c):
+            c0, c1 = 256 * c, 256 * (c + 1)
+            nc.vector.quantize_mx(
+                out=fqw[:, G, h * HALF + c0 : h * HALF + c1].bitcast(FP8X4),
+                scales=fqs[:, G, h * HALF + c0 : h * HALF + c1],
+                in_=fb[h, G][:, c0:c1, :].rearrange("p c t -> p (c t)"),
+            )
+
+        zb, qb, mx, ee, eq, qc = {}, {}, {}, {}, {}, {}
+
+        def mm_w(u, words, scales, tag):
+            i, hf = divmod(u, 2)
+            bk = bank(tag)
+            for G in range(2):
+                nc.tensor.matmul_mx(
+                    out=bk[:],
+                    lhsT=fqw[:, G, i * P : (i + 1) * P].bitcast(FP8X4),
+                    lhsT_scale=fqs[:, G, i * P : (i + 1) * P],
+                    rhs=words[:, G, hf * HALF : (hf + 1) * HALF].bitcast(FP8X4),
+                    rhs_scale=scales[4 * G : P, hf * HALF : (hf + 1) * HALF],
+                    start=(G == 0),
+                    stop=(G == 1),
+                )
+            return bk
+
+        def mmz(u):
+            zb[u] = mm_w(u, wpw, wps, "z")
+
+        def mmq(u):
+            qb[u] = mm_w(u, wqw, wqs, "q")
+
+        def unit(t, u):
+            return t[u // 2][:, :, (u % 2) * 64 : (u % 2 + 1) * 64]
+
+        def zmax(u):
+            mx[u] = work.tile([P, 64], F32, name="mx", tag="mx", bufs=4)
+            nc.vector.tensor_reduce(
+                out=mx[u][:], in_=zb[u][:].rearrange("p (o a) -> p o a", a=A), axis=AX.X, op=ALU.max
+            )
+
+        def sub(u):
+            if u // 2 not in ee:
+                ee[u // 2] = work.tile([P, A, O], F32, name="ee", tag="ee", bufs=5)
+            nc.vector.tensor_tensor(
+                out=unit(ee, u),
+                in0=zb[u][:].rearrange("p (o a) -> p a o", a=A),
+                in1=mx[u][:].unsqueeze(1).to_broadcast([P, A, 64]),
+                op=ALU.subtract,
+            )
+
+        def exp(u):
+            nc.scalar.activation(out=unit(ee, u), in_=unit(ee, u), func=ACT.Exp)
+
+        def qcp(u):
+            qc[u] = work.tile([P, A, 64], F32, name="qc", tag="qc", bufs=4)
+            nc.scalar.copy(out=qc[u][:], in_=qb[u][:].rearrange("p (o a) -> p a o", a=A))
+
+        def mul(u):
+            if u // 2 not in eq:
+                eq[u // 2] = work.tile([P, A, O], F32, name="eq", tag="eq", bufs=4)
+            if u in EQG:
+                nc.gpsimd.tensor_tensor(out=unit(eq, u), in0=qc[u][:], in1=unit(ee, u), op=ALU.mult)
+            else:
+                nc.vector.tensor_tensor(
+                    out=unit(eq, u), in0=qb[u][:].rearrange("p (o a) -> p a o", a=A), in1=unit(ee, u), op=ALU.mult
+                )
+
+        sbank, rr, qT, qo, vm, res = {}, {}, {}, {}, {}, {}
+
+        def add_up(i, s, src):
+            k, j = BANK_OF[i]
+            if k not in sbank:
+                sbank[k] = bank("s")
+            c0 = (2 * j + s) * P
+            for a in range(A):
+                nc.tensor.matmul(
+                    sbank[k][:, c0 : c0 + P],
+                    lhsT=src[:, a, :],
+                    rhs=ident[:],
+                    is_transpose=True,
+                    start=(a == 0),
+                    stop=(a == A - 1),
+                )
+
+        def sume(i):
+            add_up(i, 0, ee[i])
+
+        def sumq(i):
+            add_up(i, 1, eq[i])
+
+        def pairs(k, s):
+            i0, n, kind = GROUPS[k]
+            parts = []
+            for j0 in range(0, n, 2):
+                m = min(2, n - j0)
+                v = sbank[BANK_OF[i0 + j0][0]][:].rearrange("p (j s c) -> p j s c", s=2, c=P)
+                parts.append((j0, m, v[:, 0:m, s, :]))
+            return parts
+
+        def new_rr(k):
+            rr[k] = work.tile([P, GROUPS[k][1], P], F32, name="rr%d" % k, tag="rr%d" % k, bufs=1)
+
+        def recip(k):
+            new_rr(k)
+            for j0, m, v in pairs(k, 0):
+                nc.vector.reciprocal(out=rr[k][:, j0 : j0 + m, :], in_=v)
+
+        def ln(k):
+            new_rr(k)
+            for j0, m, v in pairs(k, 0):
+                nc.scalar.activation(out=rr[k][:, j0 : j0 + m, :], in_=v, func=ACT.Ln)
+
+        def rexp(k):
+            nc.scalar.activation(out=rr[k][:], in_=rr[k][:], func=ACT.Exp, scale=-1.0)
+
+        def qmul(k):
+            qT[k] = work.tile([P, GROUPS[k][1], P], F32, name="qT%d" % k, tag="qT%d" % k, bufs=1)
+            for j0, m, v in pairs(k, 1):
+                nc.vector.tensor_tensor(
+                    out=qT[k][:, j0 : j0 + m, :], in0=v, in1=rr[k][:, j0 : j0 + m, :], op=ALU.mult
+                )
+
+        def fturn(k):
+            qo[k] = bank("o")
+            for j in range(GROUPS[k][1]):
+                nc.tensor.transpose(qo[k][:, j * P : (j + 1) * P], qT[k][:, j, :], ident[:])
+
+        def fmax(k):
+            n = GROUPS[k][1]
+            vm[k] = work.tile([P, n], F32, name="vm%d" % k, tag="vm%d" % k, bufs=1)
+            nc.vector.tensor_reduce(
+                out=vm[k][:], in_=qo[k][:, 0 : n * P].rearrange("p (j o) -> p j o", o=O), axis=AX.X, op=ALU.max
+            )
+
+        def mix(k):
+            i0, n, kind = GROUPS[k]
+            res[k] = work.tile([P, n, O], F32, name="res%d" % k, tag="res%d" % k, bufs=1)
+            for j in range(n):
+                nc.vector.scalar_tensor_tensor(
+                    out=res[k][:, j, :],
+                    in0=qo[k][:, j * P : (j + 1) * P],
+                    scalar=vm[k][:, j : j + 1],
+                    in1=beta[:, i0 + j, :],
+                    op0=ALU.subtract,
+                    op1=ALU.mult,
+                )
+
+        def fout(k):
+            i0, n, kind = GROUPS[k]
+            for j in range(n):
+                nc.scalar.activation(
+                    out=res[k][:, j, :], in_=res[k][:, j, :], func=ACT.Identity, bias=vm[k][:, j : j + 1]
+                )
+            nc.sync.dma_start(out=out.rearrange("(n p) o -> p n o", p=P)[:, i0 : i0 + n, :], in_=res[k][:])
+
+        bbank, bsum = {}, {}
+
+        def mmb(h):
+            bbank[h] = bank(BTAG)
+            for j in range(4):
+                i = 4 * h + j
+                for G in range(2):
+                    nc.tensor.matmul_mx(
+                        out=bbank[h][:, j * O : (j + 1) * O],
+                        lhsT=fqw[:, G, i * P : (i + 1) * P].bitcast(FP8X4),
+                        lhsT_scale=fqs[:, G, i * P : (i + 1) * P],
+                        rhs=wbw[:, G, :].bitcast(FP8X4),
+                        rhs_scale=wbs[4 * G : P, :],
+                        start=(G == 0),
+                        stop=(G == 1),
+                    )
+
+        def bcp(h):
+            bsum[h] = work.tile([P, 4, O], F32, name="bsum", tag="bsum", bufs=2)
+            nc.scalar.copy(out=bsum[h][:], in_=bbank[h][:].rearrange("p (j o) -> p j o", o=O))
+
+        def bbias(h):
+            nc.gpsimd.tensor_tensor(
+                out=bsum[h][:], in0=bsum[h][:], in1=bbt[:].unsqueeze(1).to_broadcast([P, 4, O]), op=ALU.add
+            )
+
+        def btanh(h):
+            nc.scalar.activation(out=bsum[h][:], in_=bsum[h][:], func=ACT.Tanh, scale=0.5)
+
+        def baff(h):
+            nc.gpsimd.tensor_scalar(
+                out=beta[:, 4 * h : 4 * h + 4, :],
+                in0=bsum[h][:],
+                scalar1=-0.5,
+                scalar2=0.5,
+                op0=ALU.mult,
+                op1=ALU.add,
+            )
+
+        do = {
+            "pick": pick, "widen": widen, "turn": turn, "evac": evac, "quantx": quantx, "permW": permW,
+            "permS": permS, "mmf": mmf, "tanh": tanh, "gain": gain, "quantf": quantf, "mmz": mmz, "mmq": mmq,
+            "max": zmax, "sub": sub, "exp": exp, "qcp": qcp, "mul": mul, "sume": sume, "sumq": sumq,
+            "recip": recip, "ln": ln, "rexp": rexp, "qmul": qmul, "fturn": fturn, "fmax": fmax, "mix": mix,
+            "fout": fout, "mmb": mmb, "bcp": bcp, "bbias": bbias, "btanh": btanh, "baff": baff,
+        }
+        for name, args in PLAN:
+            do[name](*args)

@@ -24,249 +24,236 @@ HALF = 512
 NT = B // P
 FLOPS = 2 * B * D * F + 2 * B * F * (2 * O * A + O)
 
-WIDEN = 'VVVVVVVV'
-EVAC = 'VSVSSSSS'
+WIDEN = 'VSVSVVSV'
+EVAC = 'SSSVSSVV'
 XTAG = 'qqsoqqso'
-BUFS = {'z': 3, 'q': 2, 's': 2, 'o': 1}
+BUFS = {'z': 3, 'q': 2, 's': 2, 'o': 1, 'ee': 5, 'qc': 3}
 FTAG = ('z', 's')
 BTAG = 'o'
-EQG = (4, 5, 6, 7, 8, 9, 10, 11, 12, 13)
+EQG = (1, 2, 3, 4, 5)
 GROUPS = {0: (0, 4, 'ln'), 4: (4, 2, 'v'), 6: (6, 1, 'v'), 7: (7, 1, 'v')}
 BANK_OF = {0: (0, 0), 1: (0, 1), 2: (2, 0), 3: (2, 1), 4: (4, 0), 5: (4, 1), 6: (6, 0), 7: (7, 0)}
-GAIN = {(0, 0, 0): 'V', (0, 0, 1): 'G', (0, 1, 0): 'V', (0, 1, 1): 'G', (1, 0, 0): 'G', (1, 0, 1): 'G', (1, 1, 0): 'V', (1, 1, 1): 'G'}
+GAIN = {(0, 0, 0): 'V', (0, 0, 1): 'V', (0, 1, 0): 'V', (0, 1, 1): 'V', (1, 0, 0): 'V', (1, 0, 1): 'G', (1, 1, 0): 'G', (1, 1, 1): 'G'}
 PLAN = [
     ('widen', (0,)),
     ('widen', (1,)),
-    ('turn', (0,)),
     ('pick', ()),
+    ('turn', (0,)),
     ('widen', (2,)),
-    ('turn', (1,)),
-    ('evac', (0, 0)),
-    ('evac', (1, 0)),
     ('widen', (3,)),
-    ('evac', (0, 1)),
+    ('permS', (0,)),
+    ('turn', (1,)),
+    ('permS', (1,)),
+    ('turn', (2,)),
+    ('evac', (1, 1)),
     ('turn', (3,)),
     ('permW', (0,)),
-    ('evac', (3, 0)),
-    ('widen', (5,)),
+    ('evac', (1, 0)),
     ('evac', (3, 1)),
-    ('widen', (6,)),
-    ('turn', (5,)),
-    ('evac', (1, 1)),
-    ('widen', (7,)),
-    ('turn', (2,)),
-    ('evac', (5, 0)),
+    ('evac', (0, 0)),
     ('widen', (4,)),
-    ('turn', (6,)),
-    ('evac', (5, 1)),
-    ('evac', (2, 0)),
-    ('turn', (7,)),
-    ('evac', (6, 0)),
-    ('permS', (0,)),
-    ('turn', (4,)),
-    ('evac', (7, 0)),
     ('evac', (2, 1)),
-    ('evac', (4, 0)),
+    ('evac', (3, 0)),
+    ('evac', (2, 0)),
+    ('widen', (7,)),
+    ('evac', (0, 1)),
+    ('widen', (5,)),
+    ('widen', (6,)),
+    ('turn', (4,)),
     ('quantx', (0, 0)),
-    ('evac', (7, 1)),
+    ('turn', (5,)),
     ('quantx', (0, 1)),
-    ('evac', (6, 1)),
-    ('permS', (1,)),
-    ('mmf', (0, 0, 1)),
     ('evac', (4, 1)),
+    ('turn', (6,)),
+    ('evac', (4, 0)),
     ('permW', (1,)),
+    ('turn', (7,)),
+    ('evac', (5, 1)),
     ('mmf', (0, 0, 0)),
-    ('tanh', (0, 0, 1)),
-    ('quantx', (1, 0)),
-    ('mmf', (0, 1, 0)),
+    ('evac', (6, 0)),
+    ('evac', (5, 0)),
+    ('evac', (6, 1)),
+    ('mmf', (0, 0, 1)),
     ('tanh', (0, 0, 0)),
-    ('quantx', (1, 1)),
+    ('evac', (7, 0)),
     ('mmf', (0, 0, 2)),
-    ('tanh', (0, 1, 0)),
+    ('tanh', (0, 0, 1)),
+    ('evac', (7, 1)),
     ('mmf', (0, 0, 3)),
     ('tanh', (0, 0, 2)),
-    ('mmf', (0, 1, 3)),
+    ('mmf', (0, 1, 0)),
+    ('quantx', (1, 0)),
     ('tanh', (0, 0, 3)),
     ('mmf', (0, 1, 1)),
-    ('tanh', (0, 1, 3)),
-    ('gain', (0, 0, 0)),
-    ('gain', (0, 0, 1)),
+    ('quantx', (1, 1)),
+    ('tanh', (0, 1, 0)),
     ('mmf', (0, 1, 2)),
+    ('gain', (0, 0, 1)),
     ('tanh', (0, 1, 1)),
-    ('mmf', (1, 0, 0)),
+    ('mmf', (0, 1, 3)),
     ('tanh', (0, 1, 2)),
-    ('quantf', (0, 0, 0)),
-    ('mmf', (1, 0, 2)),
-    ('tanh', (1, 0, 0)),
-    ('gain', (0, 1, 0)),
-    ('tanh', (1, 0, 2)),
-    ('mmf', (1, 0, 3)),
-    ('gain', (0, 1, 1)),
+    ('mmf', (1, 0, 0)),
+    ('gain', (0, 0, 0)),
+    ('tanh', (0, 1, 3)),
     ('mmf', (1, 0, 1)),
+    ('tanh', (1, 0, 0)),
+    ('quantf', (0, 0, 1)),
+    ('gain', (0, 1, 0)),
+    ('tanh', (1, 0, 1)),
+    ('mmf', (1, 0, 2)),
+    ('mmf', (1, 0, 3)),
+    ('tanh', (1, 0, 2)),
+    ('quantf', (0, 0, 0)),
     ('quantf', (0, 1, 0)),
     ('tanh', (1, 0, 3)),
-    ('mmz', (0,)),
-    ('tanh', (1, 0, 1)),
-    ('mmf', (1, 1, 2)),
-    ('max', (0,)),
-    ('mmz', (3,)),
-    ('gain', (1, 0, 0)),
-    ('tanh', (1, 1, 2)),
-    ('quantf', (0, 0, 1)),
-    ('quantf', (0, 1, 1)),
-    ('mmf', (1, 1, 1)),
-    ('max', (3,)),
-    ('mmz', (5,)),
-    ('tanh', (1, 1, 1)),
-    ('sub', (0,)),
     ('mmf', (1, 1, 0)),
-    ('sub', (3,)),
-    ('mmz', (4,)),
-    ('gain', (1, 0, 1)),
+    ('gain', (0, 1, 1)),
+    ('mmz', (0,)),
     ('tanh', (1, 1, 0)),
-    ('max', (5,)),
-    ('mmf', (1, 1, 3)),
-    ('exp', (0,)),
-    ('max', (4,)),
-    ('mmq', (5,)),
-    ('tanh', (1, 1, 3)),
-    ('sub', (4,)),
-    ('mmq', (7,)),
-    ('qcp', (5,)),
-    ('quantf', (1, 0, 0)),
+    ('mmf', (1, 1, 1)),
+    ('gain', (1, 0, 0)),
     ('mmz', (1,)),
+    ('tanh', (1, 1, 1)),
+    ('mmf', (1, 1, 2)),
+    ('quantf', (0, 1, 1)),
+    ('gain', (1, 0, 1)),
+    ('max', (0,)),
+    ('mmq', (0,)),
+    ('tanh', (1, 1, 2)),
+    ('mmf', (1, 1, 3)),
+    ('max', (1,)),
+    ('mmz', (2,)),
+    ('sub', (0,)),
+    ('tanh', (1, 1, 3)),
+    ('mmb', (0,)),
+    ('sub', (1,)),
+    ('mmq', (1,)),
+    ('max', (2,)),
+    ('exp', (0,)),
     ('gain', (1, 1, 0)),
-    ('qcp', (7,)),
+    ('mmz', (3,)),
+    ('sub', (2,)),
+    ('mmz', (4,)),
+    ('bcp', (0,)),
+    ('mul', (0,)),
+    ('sume', (0,)),
+    ('max', (3,)),
+    ('mmq', (2,)),
+    ('mul', (1,)),
+    ('bbias', (0,)),
+    ('mmz', (5,)),
+    ('sub', (3,)),
+    ('qcp', (2,)),
+    ('mmq', (3,)),
+    ('max', (4,)),
+    ('exp', (1,)),
+    ('mmz', (6,)),
+    ('max', (5,)),
     ('gain', (1, 1, 1)),
     ('mmq', (4,)),
-    ('exp', (3,)),
-    ('mmb', (0,)),
-    ('max', (1,)),
-    ('qcp', (4,)),
-    ('mmq', (6,)),
+    ('sub', (4,)),
+    ('qcp', (3,)),
+    ('sume', (1,)),
     ('sub', (5,)),
-    ('mmq', (0,)),
-    ('quantf', (1, 1, 0)),
-    ('qcp', (6,)),
-    ('quantf', (1, 1, 1)),
-    ('mmz', (2,)),
-    ('sub', (1,)),
-    ('exp', (5,)),
-    ('mmz', (6,)),
-    ('max', (2,)),
-    ('exp', (4,)),
-    ('mmz', (9,)),
-    ('mul', (0,)),
-    ('bcp', (0,)),
-    ('mul', (4,)),
-    ('mmq', (8,)),
-    ('sub', (2,)),
-    ('mmq', (3,)),
-    ('qcp', (8,)),
+    ('btanh', (0,)),
     ('max', (6,)),
-    ('mmz', (8,)),
-    ('exp', (1,)),
-    ('sub', (6,)),
-    ('mmq', (1,)),
-    ('mul', (3,)),
-    ('exp', (6,)),
+    ('sumq', (0,)),
+    ('qcp', (4,)),
+    ('mmq', (5,)),
+    ('quantf', (1, 1, 0)),
     ('mmz', (7,)),
-    ('max', (9,)),
-    ('sume', (2,)),
-    ('mul', (6,)),
-    ('max', (8,)),
-    ('sume', (0,)),
-    ('sub', (9,)),
-    ('mul', (5,)),
-    ('mmq', (11,)),
-    ('sub', (8,)),
+    ('quantf', (1, 0, 0)),
+    ('qcp', (5,)),
     ('quantf', (1, 0, 1)),
-    ('mmz', (10,)),
-    ('exp', (8,)),
-    ('max', (7,)),
-    ('mmb', (1,)),
-    ('qcp', (11,)),
-    ('mul', (8,)),
-    ('sub', (7,)),
-    ('mmz', (12,)),
-    ('exp', (9,)),
-    ('mul', (1,)),
-    ('mmz', (11,)),
-    ('exp', (7,)),
-    ('max', (10,)),
-    ('mmq', (9,)),
+    ('mmq', (6,)),
+    ('quantf', (1, 1, 1)),
     ('exp', (2,)),
+    ('mulG', (1,)),
+    ('max', (7,)),
+    ('mmq', (7,)),
+    ('mmz', (8,)),
+    ('sub', (6,)),
+    ('qcp', (6,)),
+    ('mmb', (1,)),
+    ('sub', (7,)),
+    ('qcp', (7,)),
+    ('mmz', (9,)),
+    ('max', (8,)),
+    ('bcp', (1,)),
+    ('mmz', (10,)),
+    ('sub', (8,)),
+    ('exp', (3,)),
+    ('mulG', (2,)),
+    ('mmq', (8,)),
+    ('max', (9,)),
+    ('mmq', (9,)),
+    ('qcp', (8,)),
+    ('sub', (9,)),
+    ('mmz', (11,)),
+    ('max', (10,)),
+    ('exp', (4,)),
+    ('sume', (2,)),
     ('sub', (10,)),
     ('sume', (3,)),
-    ('bcp', (1,)),
-    ('max', (12,)),
-    ('exp', (10,)),
-    ('sume', (1,)),
-    ('bbias', (1,)),
+    ('mulG', (3,)),
     ('max', (11,)),
     ('qcp', (9,)),
-    ('mmz', (15,)),
-    ('sub', (12,)),
-    ('ln', (0,)),
-    ('bbias', (0,)),
+    ('mmz', (12,)),
     ('sub', (11,)),
-    ('mmq', (2,)),
-    ('mmz', (14,)),
-    ('mul', (2,)),
+    ('ln', (0,)),
+    ('mmq', (10,)),
+    ('max', (12,)),
     ('mmz', (13,)),
-    ('mul', (7,)),
-    ('max', (15,)),
-    ('sumq', (1,)),
-    ('btanh', (0,)),
+    ('sub', (12,)),
+    ('mmz', (14,)),
+    ('baff', (0,)),
     ('max', (13,)),
-    ('sumq', (0,)),
+    ('sumq', (1,)),
+    ('rexp', (0,)),
     ('sub', (13,)),
+    ('mulG', (4,)),
+    ('sumq', (2,)),
     ('max', (14,)),
     ('sumq', (3,)),
-    ('sub', (15,)),
-    ('sumq', (2,)),
-    ('rexp', (0,)),
-    ('baff', (0,)),
-    ('mmq', (10,)),
-    ('exp', (11,)),
-    ('qmul', (0,)),
-    ('mul', (9,)),
-    ('mmq', (12,)),
-    ('exp', (12,)),
     ('sub', (14,)),
+    ('mmz', (15,)),
+    ('exp', (5,)),
+    ('qmul', (0,)),
+    ('mmq', (11,)),
+    ('max', (15,)),
     ('fturn', (0,)),
     ('qcp', (10,)),
+    ('sub', (15,)),
     ('sume', (4,)),
-    ('mul', (11,)),
+    ('qcp', (11,)),
     ('fmax', (0,)),
-    ('exp', (13,)),
     ('sume', (5,)),
-    ('qcp', (12,)),
+    ('exp', (6,)),
+    ('mulG', (5,)),
     ('mix', (0,)),
-    ('mul', (10,)),
-    ('sume', (6,)),
-    ('exp', (15,)),
+    ('sumq', (4,)),
+    ('exp', (7,)),
     ('recip', (4,)),
+    ('mmq', (12,)),
     ('mmq', (13,)),
+    ('sume', (6,)),
+    ('bbias', (1,)),
     ('mul', (12,)),
     ('sumq', (5,)),
-    ('qcp', (13,)),
-    ('btanh', (1,)),
-    ('sumq', (4,)),
     ('mul', (13,)),
-    ('recip', (6,)),
-    ('exp', (14,)),
     ('mmq', (14,)),
-    ('fout', (0,)),
-    ('mmq', (15,)),
     ('qmul', (4,)),
+    ('btanh', (1,)),
+    ('recip', (6,)),
+    ('sume', (7,)),
+    ('fout', (0,)),
     ('baff', (1,)),
-    ('mul', (14,)),
     ('fturn', (4,)),
+    ('mmq', (15,)),
+    ('mul', (14,)),
+    ('fmax', (4,)),
     ('sumq', (6,)),
     ('mul', (15,)),
-    ('fmax', (4,)),
-    ('sume', (7,)),
     ('mix', (4,)),
     ('sumq', (7,)),
     ('qmul', (6,)),
@@ -295,14 +282,14 @@ def tile_optioncriticuponarrivalvalue_d2p_kernel(
 
         xsc = keep.tile([P, 64], F32, name="xsc")
         xsp = keep.tile([P, 2, NT], F32, name="xsp")
-        w0w = keep.tile([P, 2, F], I32, name="w0w", align_bytes=64)
-        w0p = keep.tile([P, 2, F], I32, name="w0p", align_bytes=64)
+        w0w = keep.tile([P, 2, 2, HALF], I32, name="w0w", align_bytes=64)
+        w0p = keep.tile([P, 2, 2, HALF], I32, name="w0p", align_bytes=64)
         w0s = keep.tile([P, F], U8, name="w0s", align_bytes=64)
         w0sp = keep.tile([P, F], U8, name="w0sp", align_bytes=64)
         gft = keep.tile([P, 2, 4], BF16, name="gft")
         bbt = keep.tile([P, O], BF16, name="bbt")
-        wpw = keep.tile([P, 2, O * A], I32, name="wpw", align_bytes=64)
-        wqw = keep.tile([P, 2, O * A], I32, name="wqw", align_bytes=64)
+        wpw = keep.tile([P, 2, 2, HALF], I32, name="wpw", align_bytes=64)
+        wqw = keep.tile([P, 2, 2, HALF], I32, name="wqw", align_bytes=64)
         wps = keep.tile([P, O * A], U8, name="wps", align_bytes=64)
         wqs = keep.tile([P, O * A], U8, name="wqs", align_bytes=64)
         wbw = keep.tile([P, 2, O], I32, name="wbw", align_bytes=64)
@@ -314,7 +301,7 @@ def tile_optioncriticuponarrivalvalue_d2p_kernel(
         fqs = keep.tile([P, 2, B], U8, name="fqs", align_bytes=64)
         beta = keep.tile([P, NT, O], F32, name="beta")
         dummy = keep.tile([P, 1], F32, name="dummy")
-        xb = [keep.tile([P, D], U8, name="xb%d" % i) for i in range(NT)]
+        xall = keep.tile([P, NT, D], U8, name="xall")
 
         ctx.enter_context(tc.manual_schedule())
 
@@ -326,8 +313,10 @@ def tile_optioncriticuponarrivalvalue_d2p_kernel(
         nc.gpsimd.memset(wqs[:].bitcast(I32), 0)
         nc.gpsimd.memset(wbs[:].bitcast(I32), 0)
 
-        def load_x(i):
-            nc.sync.dma_start(out=xb[i][:], in_=x_bytes[i * P : (i + 1) * P, :])
+        def load_x(i0, n):
+            nc.sync.dma_start(
+                out=xall[:, i0 : i0 + n, :], in_=x_bytes.rearrange("(i p) d -> p i d", p=P)[:, i0 : i0 + n, :]
+            )
 
         def load_scales(dst, src):
             for q in range(4):
@@ -336,34 +325,28 @@ def tile_optioncriticuponarrivalvalue_d2p_kernel(
                     in_=src[:, 4 * q : 4 * q + 4, :].bitcast(I32),
                 )
 
-        def load_words(dst, src, g, c0, c1):
+        def load_words(dst, src, c0, c1):
             nc.sync.dma_start(
-                out=dst[:, g, c0:c1],
-                in_=src[g].rearrange("p n t -> p (n t)")[:, 4 * c0 : 4 * c1].bitcast(I32),
+                out=dst,
+                in_=src.rearrange("g p n t -> p g (n t)")[:, :, 4 * c0 : 4 * c1].bitcast(I32),
             )
 
-        load_x(0)
+        load_x(0, 1)
         nc.sync.dma_start(out=xsc[:], in_=x_scale.rearrange("i j -> (i j)").partition_broadcast(P))
-        for i in range(1, 4):
-            load_x(i)
+        load_x(1, 1)
+        load_x(2, 2)
         load_scales(w0s, w0_scales)
-        for g in range(2):
-            load_words(w0w, w0_words, g, 0, HALF)
+        load_words(w0w[:, 0], w0_words, 0, HALF)
+        load_x(4, 4)
+        load_words(w0w[:, 1], w0_words, HALF, F)
         nc.sync.dma_start(out=gft[:], in_=gf.rearrange("(g p t) -> p g t", p=P, t=4))
         load_scales(wps, wp_scales)
         load_scales(wqs, wq_scales)
-        load_scales(wbs, wb_scales)
-        for i in range(4, NT):
-            load_x(i)
-        for g in range(2):
-            load_words(w0w, w0_words, g, HALF, F)
         for c in range(2):
-            for g in range(2):
-                load_words(wpw, wp_words, g, c * HALF, (c + 1) * HALF)
-            for g in range(2):
-                load_words(wqw, wq_words, g, c * HALF, (c + 1) * HALF)
-        for g in range(2):
-            load_words(wbw, wb_words, g, 0, O)
+            load_words(wpw[:, c], wp_words, c * HALF, (c + 1) * HALF)
+            load_words(wqw[:, c], wq_words, c * HALF, (c + 1) * HALF)
+        load_scales(wbs, wb_scales)
+        load_words(wbw[:], wb_words, 0, O)
         nc.sync.dma_start(out=bbt[:], in_=bb.partition_broadcast(P))
 
         def bank(tag):
@@ -383,7 +366,7 @@ def tile_optioncriticuponarrivalvalue_d2p_kernel(
 
         def widen(i):
             t = work.tile([P, D], BF16, name="xw", tag="xw", bufs=8, align_bytes=64)
-            src = xb[i][:].bitcast(FP8)
+            src = xall[:, i, :].bitcast(FP8)
             if WIDEN[i] == "V":
                 nc.vector.tensor_copy(out=t[:], in_=src)
             else:
@@ -421,8 +404,8 @@ def tile_optioncriticuponarrivalvalue_d2p_kernel(
 
         def permW(G):
             nc.vector.tensor_copy(
-                out=w0p[:, :, G * HALF : (G + 1) * HALF].rearrange("p g (t m) -> p g t m", t=4),
-                in_=w0w[:, :, G * HALF : (G + 1) * HALF].rearrange("p g (m t) -> p g t m", t=4),
+                out=w0p[:, G].rearrange("p g (t m) -> p g t m", t=4),
+                in_=w0w[:, G].rearrange("p g (m t) -> p g t m", t=4),
             )
 
         def permS(G):
@@ -439,7 +422,7 @@ def tile_optioncriticuponarrivalvalue_d2p_kernel(
             for g in range(2):
                 nc.tensor.matmul_mx(
                     out=bk[:],
-                    lhsT=w0p[:, g, c0 : c0 + P].bitcast(FP8X4),
+                    lhsT=w0p[:, G, g, t * P : (t + 1) * P].bitcast(FP8X4),
                     lhsT_scale=w0sp[4 * g : P, c0 : c0 + P],
                     rhs=xqw[:, g, h * HALF : (h + 1) * HALF].bitcast(FP8X4),
                     rhs_scale=xqs[:, g, h * HALF : (h + 1) * HALF],
@@ -483,7 +466,7 @@ def tile_optioncriticuponarrivalvalue_d2p_kernel(
                     out=bk[:],
                     lhsT=fqw[:, G, i * P : (i + 1) * P].bitcast(FP8X4),
                     lhsT_scale=fqs[:, G, i * P : (i + 1) * P],
-                    rhs=words[:, G, hf * HALF : (hf + 1) * HALF].bitcast(FP8X4),
+                    rhs=words[:, hf, G, :].bitcast(FP8X4),
                     rhs_scale=scales[4 * G : P, hf * HALF : (hf + 1) * HALF],
                     start=(G == 0),
                     stop=(G == 1),
@@ -515,22 +498,28 @@ def tile_optioncriticuponarrivalvalue_d2p_kernel(
                 op=ALU.subtract,
             )
 
-        def exp(u):
-            nc.scalar.activation(out=unit(ee, u), in_=unit(ee, u), func=ACT.Exp)
+        def exp(i):
+            v = ee[i][:].rearrange("p a o -> p (a o)")
+            nc.scalar.activation(out=v, in_=v, func=ACT.Exp)
 
         def qcp(u):
-            qc[u] = work.tile([P, A, 64], F32, name="qc", tag="qc", bufs=4)
-            nc.scalar.copy(out=qc[u][:], in_=qb[u][:].rearrange("p (o a) -> p a o", a=A))
+            if u // 2 not in qc:
+                qc[u // 2] = work.tile([P, A, O], F32, name="qc", tag="qc", bufs=3)
+            nc.scalar.copy(out=unit(qc, u), in_=qb[u][:].rearrange("p (o a) -> p a o", a=A))
+
+        def new_eq(i):
+            if i not in eq:
+                eq[i] = work.tile([P, A, O], F32, name="eq", tag="eq", bufs=6)
+
+        def mulG(i):
+            new_eq(i)
+            nc.gpsimd.tensor_tensor(out=eq[i][:], in0=qc[i][:], in1=ee[i][:], op=ALU.mult)
 
         def mul(u):
-            if u // 2 not in eq:
-                eq[u // 2] = work.tile([P, A, O], F32, name="eq", tag="eq", bufs=4)
-            if u in EQG:
-                nc.gpsimd.tensor_tensor(out=unit(eq, u), in0=qc[u][:], in1=unit(ee, u), op=ALU.mult)
-            else:
-                nc.vector.tensor_tensor(
-                    out=unit(eq, u), in0=qb[u][:].rearrange("p (o a) -> p a o", a=A), in1=unit(ee, u), op=ALU.mult
-                )
+            new_eq(u // 2)
+            nc.vector.tensor_tensor(
+                out=unit(eq, u), in0=qb[u][:].rearrange("p (o a) -> p a o", a=A), in1=unit(ee, u), op=ALU.mult
+            )
 
         sbank, rr, qT, qo, vm, res = {}, {}, {}, {}, {}, {}
 
@@ -662,7 +651,7 @@ def tile_optioncriticuponarrivalvalue_d2p_kernel(
         do = {
             "pick": pick, "widen": widen, "turn": turn, "evac": evac, "quantx": quantx, "permW": permW,
             "permS": permS, "mmf": mmf, "tanh": tanh, "gain": gain, "quantf": quantf, "mmz": mmz, "mmq": mmq,
-            "max": zmax, "sub": sub, "exp": exp, "qcp": qcp, "mul": mul, "sume": sume, "sumq": sumq,
+            "max": zmax, "sub": sub, "exp": exp, "qcp": qcp, "mul": mul, "mulG": mulG, "sume": sume, "sumq": sumq,
             "recip": recip, "ln": ln, "rexp": rexp, "qmul": qmul, "fturn": fturn, "fmax": fmax, "mix": mix,
             "fout": fout, "mmb": mmb, "bcp": bcp, "bbias": bbias, "btanh": btanh, "baff": baff,
         }

from contextlib import ExitStack

import concourse.mybir as mybir
from concourse.masks import make_identity

F32 = mybir.dt.float32
BF16 = mybir.dt.bfloat16
I32 = mybir.dt.int32
U32 = mybir.dt.uint32
U8 = mybir.dt.uint8
FP8 = mybir.dt.float8_e4m3fn
FP8X4 = mybir.dt.float8_e4m3fn_x4
ALU = mybir.AluOpType
ACT = mybir.ActivationFunctionType
AX = mybir.AxisListType

P = 128
B = 1024
D = 1024
F = 1024
O = 128
A = 8
HALF = 512
NT = B // P
FLOPS = 2 * B * D * F + 2 * B * F * (2 * O * A + O)

WIDEN = 'VSVSVVSV'
EVAC = 'SSSVSSVV'
XTAG = 'qqsoqqso'
BUFS = {'z': 3, 'q': 2, 's': 2, 'o': 1, 'ee': 5, 'qc': 3}
FTAG = ('z', 's')
BTAG = 'o'
EQG = (1, 2, 3, 4, 5)
GROUPS = {0: (0, 4, 'ln'), 4: (4, 2, 'v'), 6: (6, 1, 'v'), 7: (7, 1, 'v')}
BANK_OF = {0: (0, 0), 1: (0, 1), 2: (2, 0), 3: (2, 1), 4: (4, 0), 5: (4, 1), 6: (6, 0), 7: (7, 0)}
GAIN = {(0, 0, 0): 'V', (0, 0, 1): 'V', (0, 1, 0): 'V', (0, 1, 1): 'V', (1, 0, 0): 'V', (1, 0, 1): 'G', (1, 1, 0): 'G', (1, 1, 1): 'G'}
PLAN = [
    ('widen', (0,)),
    ('widen', (1,)),
    ('pick', ()),
    ('turn', (0,)),
    ('widen', (2,)),
    ('widen', (3,)),
    ('permS', (0,)),
    ('turn', (1,)),
    ('permS', (1,)),
    ('turn', (2,)),
    ('evac', (1, 1)),
    ('turn', (3,)),
    ('permW', (0,)),
    ('evac', (1, 0)),
    ('evac', (3, 1)),
    ('evac', (0, 0)),
    ('widen', (4,)),
    ('evac', (2, 1)),
    ('evac', (3, 0)),
    ('evac', (2, 0)),
    ('widen', (7,)),
    ('evac', (0, 1)),
    ('widen', (5,)),
    ('widen', (6,)),
    ('turn', (4,)),
    ('quantx', (0, 0)),
    ('turn', (5,)),
    ('quantx', (0, 1)),
    ('evac', (4, 1)),
    ('turn', (6,)),
    ('evac', (4, 0)),
    ('permW', (1,)),
    ('turn', (7,)),
    ('evac', (5, 1)),
    ('mmf', (0, 0, 0)),
    ('evac', (6, 0)),
    ('evac', (5, 0)),
    ('evac', (6, 1)),
    ('mmf', (0, 0, 1)),
    ('tanh', (0, 0, 0)),
    ('evac', (7, 0)),
    ('mmf', (0, 0, 2)),
    ('tanh', (0, 0, 1)),
    ('evac', (7, 1)),
    ('mmf', (0, 0, 3)),
    ('tanh', (0, 0, 2)),
    ('mmf', (0, 1, 0)),
    ('quantx', (1, 0)),
    ('tanh', (0, 0, 3)),
    ('mmf', (0, 1, 1)),
    ('quantx', (1, 1)),
    ('tanh', (0, 1, 0)),
    ('mmf', (0, 1, 2)),
    ('gain', (0, 0, 1)),
    ('tanh', (0, 1, 1)),
    ('mmf', (0, 1, 3)),
    ('tanh', (0, 1, 2)),
    ('mmf', (1, 0, 0)),
    ('gain', (0, 0, 0)),
    ('tanh', (0, 1, 3)),
    ('mmf', (1, 0, 1)),
    ('tanh', (1, 0, 0)),
    ('quantf', (0, 0, 1)),
    ('gain', (0, 1, 0)),
    ('tanh', (1, 0, 1)),
    ('mmf', (1, 0, 2)),
    ('mmf', (1, 0, 3)),
    ('tanh', (1, 0, 2)),
    ('quantf', (0, 0, 0)),
    ('quantf', (0, 1, 0)),
    ('tanh', (1, 0, 3)),
    ('mmf', (1, 1, 0)),
    ('gain', (0, 1, 1)),
    ('mmz', (0,)),
    ('tanh', (1, 1, 0)),
    ('mmf', (1, 1, 1)),
    ('gain', (1, 0, 0)),
    ('mmz', (1,)),
    ('tanh', (1, 1, 1)),
    ('mmf', (1, 1, 2)),
    ('quantf', (0, 1, 1)),
    ('gain', (1, 0, 1)),
    ('max', (0,)),
    ('mmq', (0,)),
    ('tanh', (1, 1, 2)),
    ('mmf', (1, 1, 3)),
    ('max', (1,)),
    ('mmz', (2,)),
    ('sub', (0,)),
    ('tanh', (1, 1, 3)),
    ('mmb', (0,)),
    ('sub', (1,)),
    ('mmq', (1,)),
    ('max', (2,)),
    ('exp', (0,)),
    ('gain', (1, 1, 0)),
    ('mmz', (3,)),
    ('sub', (2,)),
    ('mmz', (4,)),
    ('bcp', (0,)),
    ('mul', (0,)),
    ('sume', (0,)),
    ('max', (3,)),
    ('mmq', (2,)),
    ('mul', (1,)),
    ('bbias', (0,)),
    ('mmz', (5,)),
    ('sub', (3,)),
    ('qcp', (2,)),
    ('mmq', (3,)),
    ('max', (4,)),
    ('exp', (1,)),
    ('mmz', (6,)),
    ('max', (5,)),
    ('gain', (1, 1, 1)),
    ('mmq', (4,)),
    ('sub', (4,)),
    ('qcp', (3,)),
    ('sume', (1,)),
    ('sub', (5,)),
    ('btanh', (0,)),
    ('max', (6,)),
    ('sumq', (0,)),
    ('qcp', (4,)),
    ('mmq', (5,)),
    ('quantf', (1, 1, 0)),
    ('mmz', (7,)),
    ('quantf', (1, 0, 0)),
    ('qcp', (5,)),
    ('quantf', (1, 0, 1)),
    ('mmq', (6,)),
    ('quantf', (1, 1, 1)),
    ('exp', (2,)),
    ('mulG', (1,)),
    ('max', (7,)),
    ('mmq', (7,)),
    ('mmz', (8,)),
    ('sub', (6,)),
    ('qcp', (6,)),
    ('mmb', (1,)),
    ('sub', (7,)),
    ('qcp', (7,)),
    ('mmz', (9,)),
    ('max', (8,)),
    ('bcp', (1,)),
    ('mmz', (10,)),
    ('sub', (8,)),
    ('exp', (3,)),
    ('mulG', (2,)),
    ('mmq', (8,)),
    ('max', (9,)),
    ('mmq', (9,)),
    ('qcp', (8,)),
    ('sub', (9,)),
    ('mmz', (11,)),
    ('max', (10,)),
    ('exp', (4,)),
    ('sume', (2,)),
    ('sub', (10,)),
    ('sume', (3,)),
    ('mulG', (3,)),
    ('max', (11,)),
    ('qcp', (9,)),
    ('mmz', (12,)),
    ('sub', (11,)),
    ('ln', (0,)),
    ('mmq', (10,)),
    ('max', (12,)),
    ('mmz', (13,)),
    ('sub', (12,)),
    ('mmz', (14,)),
    ('baff', (0,)),
    ('max', (13,)),
    ('sumq', (1,)),
    ('rexp', (0,)),
    ('sub', (13,)),
    ('mulG', (4,)),
    ('sumq', (2,)),
    ('max', (14,)),
    ('sumq', (3,)),
    ('sub', (14,)),
    ('mmz', (15,)),
    ('exp', (5,)),
    ('qmul', (0,)),
    ('mmq', (11,)),
    ('max', (15,)),
    ('fturn', (0,)),
    ('qcp', (10,)),
    ('sub', (15,)),
    ('sume', (4,)),
    ('qcp', (11,)),
    ('fmax', (0,)),
    ('sume', (5,)),
    ('exp', (6,)),
    ('mulG', (5,)),
    ('mix', (0,)),
    ('sumq', (4,)),
    ('exp', (7,)),
    ('recip', (4,)),
    ('mmq', (12,)),
    ('mmq', (13,)),
    ('sume', (6,)),
    ('bbias', (1,)),
    ('mul', (12,)),
    ('sumq', (5,)),
    ('mul', (13,)),
    ('mmq', (14,)),
    ('qmul', (4,)),
    ('btanh', (1,)),
    ('recip', (6,)),
    ('sume', (7,)),
    ('fout', (0,)),
    ('baff', (1,)),
    ('fturn', (4,)),
    ('mmq', (15,)),
    ('mul', (14,)),
    ('fmax', (4,)),
    ('sumq', (6,)),
    ('mul', (15,)),
    ('mix', (4,)),
    ('sumq', (7,)),
    ('qmul', (6,)),
    ('recip', (7,)),
    ('fturn', (6,)),
    ('fmax', (6,)),
    ('qmul', (7,)),
    ('mix', (6,)),
    ('fturn', (7,)),
    ('fout', (6,)),
    ('fout', (4,)),
    ('fmax', (7,)),
    ('mix', (7,)),
    ('fout', (7,)),
]


def tile_optioncriticuponarrivalvalue_d2p_kernel(
    tc, x_bytes, x_scale, w0_words, w0_scales, gf, wq_words, wq_scales, wp_words, wp_scales, wb_words, wb_scales, bb, out
):
    nc = tc.nc
    with ExitStack() as ctx:
        keep = ctx.enter_context(tc.tile_pool(name="keep", bufs=1))
        work = ctx.enter_context(tc.tile_pool(name="work", bufs=2))
        psum = ctx.enter_context(tc.psum_pool(name="psum", bufs=1))

        xsc = keep.tile([P, 64], F32, name="xsc")
        xsp = keep.tile([P, 2, NT], F32, name="xsp")
        w0w = keep.tile([P, 2, 2, HALF], I32, name="w0w", align_bytes=64)
        w0p = keep.tile([P, 2, 2, HALF], I32, name="w0p", align_bytes=64)
        w0s = keep.tile([P, F], U8, name="w0s", align_bytes=64)
        w0sp = keep.tile([P, F], U8, name="w0sp", align_bytes=64)
        gft = keep.tile([P, 2, 4], BF16, name="gft")
        bbt = keep.tile([P, O], BF16, name="bbt")
        wpw = keep.tile([P, 2, 2, HALF], I32, name="wpw", align_bytes=64)
        wqw = keep.tile([P, 2, 2, HALF], I32, name="wqw", align_bytes=64)
        wps = keep.tile([P, O * A], U8, name="wps", align_bytes=64)
        wqs = keep.tile([P, O * A], U8, name="wqs", align_bytes=64)
        wbw = keep.tile([P, 2, O], I32, name="wbw", align_bytes=64)
        wbs = keep.tile([P, O], U8, name="wbs", align_bytes=64)
        ident = keep.tile([P, P], F32, name="ident")
        xqw = keep.tile([P, 2, B], U32, name="xqw", align_bytes=64)
        xqs = keep.tile([P, 2, B], U8, name="xqs", align_bytes=64)
        fqw = keep.tile([P, 2, B], U32, name="fqw", align_bytes=64)
        fqs = keep.tile([P, 2, B], U8, name="fqs", align_bytes=64)
        beta = keep.tile([P, NT, O], F32, name="beta")
        dummy = keep.tile([P, 1], F32, name="dummy")
        xall = keep.tile([P, NT, D], U8, name="xall")

        ctx.enter_context(tc.manual_schedule())

        nc.vector.memset(dummy[:], 0.0)
        nc.scalar.activation(out=dummy[:], in_=dummy[:], func=ACT.Exp)
        nc.vector.memset(w0s[:].bitcast(I32), 0)
        make_identity(nc, ident[:])
        nc.gpsimd.memset(wps[:].bitcast(I32), 0)
        nc.gpsimd.memset(wqs[:].bitcast(I32), 0)
        nc.gpsimd.memset(wbs[:].bitcast(I32), 0)

        def load_x(i0, n):
            nc.sync.dma_start(
                out=xall[:, i0 : i0 + n, :], in_=x_bytes.rearrange("(i p) d -> p i d", p=P)[:, i0 : i0 + n, :]
            )

        def load_scales(dst, src):
            for q in range(4):
                nc.sync.dma_start(
                    out=dst[32 * q : 32 * q + 8, :].bitcast(I32),
                    in_=src[:, 4 * q : 4 * q + 4, :].bitcast(I32),
                )

        def load_words(dst, src, c0, c1):
            nc.sync.dma_start(
                out=dst,
                in_=src.rearrange("g p n t -> p g (n t)")[:, :, 4 * c0 : 4 * c1].bitcast(I32),
            )

        load_x(0, 1)
        nc.sync.dma_start(out=xsc[:], in_=x_scale.rearrange("i j -> (i j)").partition_broadcast(P))
        load_x(1, 1)
        load_x(2, 2)
        load_scales(w0s, w0_scales)
        load_words(w0w[:, 0], w0_words, 0, HALF)
        load_x(4, 4)
        load_words(w0w[:, 1], w0_words, HALF, F)
        nc.sync.dma_start(out=gft[:], in_=gf.rearrange("(g p t) -> p g t", p=P, t=4))
        load_scales(wps, wp_scales)
        load_scales(wqs, wq_scales)
        for c in range(2):
            load_words(wpw[:, c], wp_words, c * HALF, (c + 1) * HALF)
            load_words(wqw[:, c], wq_words, c * HALF, (c + 1) * HALF)
        load_scales(wbs, wb_scales)
        load_words(wbw[:], wb_words, 0, O)
        nc.sync.dma_start(out=bbt[:], in_=bb.partition_broadcast(P))

        def bank(tag):
            return psum.tile([P, HALF], F32, name="ps_" + tag, tag=tag, bufs=BUFS[tag])

        xwide, xbank, xt = {}, {}, {}
        for h in range(2):
            for g in range(2):
                xt[h, g] = keep.tile([P, HALF, 4], BF16, name="xt%d%d" % (h, g), align_bytes=64)

        def pick():
            for q in range(4):
                nc.vector.tensor_copy(
                    out=xsp[32 * q : 32 * q + 32, :, :],
                    in_=xsc[32 * q : 32 * q + 32, :].rearrange("p (i g q) -> p q g i", g=2, q=4)[:, q],
                )

        def widen(i):
            t = work.tile([P, D], BF16, name="xw", tag="xw", bufs=8, align_bytes=64)
            src = xall[:, i, :].bitcast(FP8)
            if WIDEN[i] == "V":
                nc.vector.tensor_copy(out=t[:], in_=src)
            else:
                nc.scalar.copy(out=t[:], in_=src)
            xwide[i] = t

        def turn(i):
            bk = bank(XTAG[i])
            words = xwide[i][:].bitcast(F32)
            for g in range(2):
                for u in range(2):
                    j = 2 * g + u
                    nc.tensor.transpose(
                        bk[:, j * P : (j + 1) * P], words[:, 256 * g + u : 256 * (g + 1) : 2], ident[:]
                    )
            xbank[i] = bk

        def evac(i, g):
            r0 = (i % 4) * P
            src = xbank[i][:, g * 256 : (g + 1) * 256].bitcast(BF16).rearrange("p (u r e) -> p r u e", u=2, e=2)
            dst = xt[i // 4, g][:, r0 : r0 + P, :].rearrange("p r (u e) -> p r u e", e=2)
            if EVAC[i] == "V":
                nc.vector.tensor_scalar(
                    out=dst, in0=src, scalar1=xsp[:, g, i : i + 1], scalar2=None, op0=ALU.mult
                )
            else:
                nc.scalar.activation(out=dst, in_=src, func=ACT.Copy, scale=xsp[:, g, i : i + 1])

        def quantx(h, g):
            nc.vector.quantize_mx(
                out=xqw[:, g, h * HALF : (h + 1) * HALF].bitcast(FP8X4),
                scales=xqs[:, g, h * HALF : (h + 1) * HALF],
                in_=xt[h, g][:].rearrange("p r t -> p (r t)"),
            )

        def permW(G):
            nc.vector.tensor_copy(
                out=w0p[:, G].rearrange("p g (t m) -> p g t m", t=4),
                in_=w0w[:, G].rearrange("p g (m t) -> p g t m", t=4),
            )

        def permS(G):
            nc.vector.tensor_copy(
                out=w0sp[:, G * HALF : (G + 1) * HALF].rearrange("p (t m) -> p t m", t=4),
                in_=w0s[:, G * HALF : (G + 1) * HALF].rearrange("p (m t) -> p t m", t=4),
            )

        fbank, th, fb = {}, {}, {}

        def mmf(h, G, t):
            bk = bank(FTAG[h])
            c0 = G * HALF + t * P
            for g in range(2):
                nc.tensor.matmul_mx(
                    out=bk[:],
                    lhsT=w0p[:, G, g, t * P : (t + 1) * P].bitcast(FP8X4),
                    lhsT_scale=w0sp[4 * g : P, c0 : c0 + P],
                    rhs=xqw[:, g, h * HALF : (h + 1) * HALF].bitcast(FP8X4),
                    rhs_scale=xqs[:, g, h * HALF : (h + 1) * HALF],
                    start=(g == 0),
                    stop=(g == 1),
                )
            fbank[h, G, t] = bk

        def tanh(h, G, t):
            if (h, G) not in th:
                th[h, G] = work.tile([P, 4, HALF], F32, name="th", tag="th", bufs=4)
            nc.scalar.activation(out=th[h, G][:, t, :], in_=fbank[h, G, t][:], func=ACT.Tanh)

        def gain(h, G, c):
            c0, c1 = 256 * c, 256 * (c + 1)
            if (h, G) not in fb:
                fb[h, G] = work.tile([P, HALF, 4], BF16, name="fb", tag="fb", bufs=4, align_bytes=64)
            eng = nc.vector if GAIN[h, G, c] == "V" else nc.gpsimd
            eng.tensor_tensor(
                out=fb[h, G][:, c0:c1, :],
                in0=th[h, G][:, :, c0:c1].rearrange("p t c -> p c t"),
                in1=gft[:, G : G + 1, :].to_broadcast([P, c1 - c0, 4]),
                op=ALU.mult,
            )

        def quantf(h, G, c):
            c0, c1 = 256 * c, 256 * (c + 1)
            nc.vector.quantize_mx(
                out=fqw[:, G, h * HALF + c0 : h * HALF + c1].bitcast(FP8X4),
                scales=fqs[:, G, h * HALF + c0 : h * HALF + c1],
                in_=fb[h, G][:, c0:c1, :].rearrange("p c t -> p (c t)"),
            )

        zb, qb, mx, ee, eq, qc = {}, {}, {}, {}, {}, {}

        def mm_w(u, words, scales, tag):
            i, hf = divmod(u, 2)
            bk = bank(tag)
            for G in range(2):
                nc.tensor.matmul_mx(
                    out=bk[:],
                    lhsT=fqw[:, G, i * P : (i + 1) * P].bitcast(FP8X4),
                    lhsT_scale=fqs[:, G, i * P : (i + 1) * P],
                    rhs=words[:, hf, G, :].bitcast(FP8X4),
                    rhs_scale=scales[4 * G : P, hf * HALF : (hf + 1) * HALF],
                    start=(G == 0),
                    stop=(G == 1),
                )
            return bk

        def mmz(u):
            zb[u] = mm_w(u, wpw, wps, "z")

        def mmq(u):
            qb[u] = mm_w(u, wqw, wqs, "q")

        def unit(t, u):
            return t[u // 2][:, :, (u % 2) * 64 : (u % 2 + 1) * 64]

        def zmax(u):
            mx[u] = work.tile([P, 64], F32, name="mx", tag="mx", bufs=4)
            nc.vector.tensor_reduce(
                out=mx[u][:], in_=zb[u][:].rearrange("p (o a) -> p o a", a=A), axis=AX.X, op=ALU.max
            )

        def sub(u):
            if u // 2 not in ee:
                ee[u // 2] = work.tile([P, A, O], F32, name="ee", tag="ee", bufs=5)
            nc.vector.tensor_tensor(
                out=unit(ee, u),
                in0=zb[u][:].rearrange("p (o a) -> p a o", a=A),
                in1=mx[u][:].unsqueeze(1).to_broadcast([P, A, 64]),
                op=ALU.subtract,
            )

        def exp(i):
            v = ee[i][:].rearrange("p a o -> p (a o)")
            nc.scalar.activation(out=v, in_=v, func=ACT.Exp)

        def qcp(u):
            if u // 2 not in qc:
                qc[u // 2] = work.tile([P, A, O], F32, name="qc", tag="qc", bufs=3)
            nc.scalar.copy(out=unit(qc, u), in_=qb[u][:].rearrange("p (o a) -> p a o", a=A))

        def new_eq(i):
            if i not in eq:
                eq[i] = work.tile([P, A, O], F32, name="eq", tag="eq", bufs=6)

        def mulG(i):
            new_eq(i)
            nc.gpsimd.tensor_tensor(out=eq[i][:], in0=qc[i][:], in1=ee[i][:], op=ALU.mult)

        def mul(u):
            new_eq(u // 2)
            nc.vector.tensor_tensor(
                out=unit(eq, u), in0=qb[u][:].rearrange("p (o a) -> p a o", a=A), in1=unit(ee, u), op=ALU.mult
            )

        sbank, rr, qT, qo, vm, res = {}, {}, {}, {}, {}, {}

        def add_up(i, s, src):
            k, j = BANK_OF[i]
            if k not in sbank:
                sbank[k] = bank("s")
            c0 = (2 * j + s) * P
            for a in range(A):
                nc.tensor.matmul(
                    sbank[k][:, c0 : c0 + P],
                    lhsT=src[:, a, :],
                    rhs=ident[:],
                    is_transpose=True,
                    start=(a == 0),
                    stop=(a == A - 1),
                )

        def sume(i):
            add_up(i, 0, ee[i])

        def sumq(i):
            add_up(i, 1, eq[i])

        def pairs(k, s):
            i0, n, kind = GROUPS[k]
            parts = []
            for j0 in range(0, n, 2):
                m = min(2, n - j0)
                v = sbank[BANK_OF[i0 + j0][0]][:].rearrange("p (j s c) -> p j s c", s=2, c=P)
                parts.append((j0, m, v[:, 0:m, s, :]))
            return parts

        def new_rr(k):
            rr[k] = work.tile([P, GROUPS[k][1], P], F32, name="rr%d" % k, tag="rr%d" % k, bufs=1)

        def recip(k):
            new_rr(k)
            for j0, m, v in pairs(k, 0):
                nc.vector.reciprocal(out=rr[k][:, j0 : j0 + m, :], in_=v)

        def ln(k):
            new_rr(k)
            for j0, m, v in pairs(k, 0):
                nc.scalar.activation(out=rr[k][:, j0 : j0 + m, :], in_=v, func=ACT.Ln)

        def rexp(k):
            nc.scalar.activation(out=rr[k][:], in_=rr[k][:], func=ACT.Exp, scale=-1.0)

        def qmul(k):
            qT[k] = work.tile([P, GROUPS[k][1], P], F32, name="qT%d" % k, tag="qT%d" % k, bufs=1)
            for j0, m, v in pairs(k, 1):
                nc.vector.tensor_tensor(
                    out=qT[k][:, j0 : j0 + m, :], in0=v, in1=rr[k][:, j0 : j0 + m, :], op=ALU.mult
                )

        def fturn(k):
            qo[k] = bank("o")
            for j in range(GROUPS[k][1]):
                nc.tensor.transpose(qo[k][:, j * P : (j + 1) * P], qT[k][:, j, :], ident[:])

        def fmax(k):
            n = GROUPS[k][1]
            vm[k] = work.tile([P, n], F32, name="vm%d" % k, tag="vm%d" % k, bufs=1)
            nc.vector.tensor_reduce(
                out=vm[k][:], in_=qo[k][:, 0 : n * P].rearrange("p (j o) -> p j o", o=O), axis=AX.X, op=ALU.max
            )

        def mix(k):
            i0, n, kind = GROUPS[k]
            res[k] = work.tile([P, n, O], F32, name="res%d" % k, tag="res%d" % k, bufs=1)
            for j in range(n):
                nc.vector.scalar_tensor_tensor(
                    out=res[k][:, j, :],
                    in0=qo[k][:, j * P : (j + 1) * P],
                    scalar=vm[k][:, j : j + 1],
                    in1=beta[:, i0 + j, :],
                    op0=ALU.subtract,
                    op1=ALU.mult,
                )

        def fout(k):
            i0, n, kind = GROUPS[k]
            for j in range(n):
                nc.scalar.activation(
                    out=res[k][:, j, :], in_=res[k][:, j, :], func=ACT.Identity, bias=vm[k][:, j : j + 1]
                )
            nc.sync.dma_start(out=out.rearrange("(n p) o -> p n o", p=P)[:, i0 : i0 + n, :], in_=res[k][:])

        bbank, bsum = {}, {}

        def mmb(h):
            bbank[h] = bank(BTAG)
            for j in range(4):
                i = 4 * h + j
                for G in range(2):
                    nc.tensor.matmul_mx(
                        out=bbank[h][:, j * O : (j + 1) * O],
                        lhsT=fqw[:, G, i * P : (i + 1) * P].bitcast(FP8X4),
                        lhsT_scale=fqs[:, G, i * P : (i + 1) * P],
                        rhs=wbw[:, G, :].bitcast(FP8X4),
                        rhs_scale=wbs[4 * G : P, :],
                        start=(G == 0),
                        stop=(G == 1),
                    )

        def bcp(h):
            bsum[h] = work.tile([P, 4, O], F32, name="bsum", tag="bsum", bufs=2)
            nc.scalar.copy(out=bsum[h][:], in_=bbank[h][:].rearrange("p (j o) -> p j o", o=O))

        def bbias(h):
            nc.gpsimd.tensor_tensor(
                out=bsum[h][:], in0=bsum[h][:], in1=bbt[:].unsqueeze(1).to_broadcast([P, 4, O]), op=ALU.add
            )

        def btanh(h):
            nc.scalar.activation(out=bsum[h][:], in_=bsum[h][:], func=ACT.Tanh, scale=0.5)

        def baff(h):
            nc.gpsimd.tensor_scalar(
                out=beta[:, 4 * h : 4 * h + 4, :],
                in0=bsum[h][:],
                scalar1=-0.5,
                scalar2=0.5,
                op0=ALU.mult,
                op1=ALU.add,
            )

        do = {
            "pick": pick, "widen": widen, "turn": turn, "evac": evac, "quantx": quantx, "permW": permW,
            "permS": permS, "mmf": mmf, "tanh": tanh, "gain": gain, "quantf": quantf, "mmz": mmz, "mmq": mmq,
            "max": zmax, "sub": sub, "exp": exp, "qcp": qcp, "mul": mul, "mulG": mulG, "sume": sume, "sumq": sumq,
            "recip": recip, "ln": ln, "rexp": rexp, "qmul": qmul, "fturn": fturn, "fmax": fmax, "mix": mix,
            "fout": fout, "mmb": mmb, "bcp": bcp, "bbias": bbias, "btanh": btanh, "baff": baff,
        }
        for name, args in PLAN:
            do[name](*args)
